import numpy as np
import ml_dtypes


def mxq(x, axis, fmt="e4m3"):
    dtype, down = {"e4m3": (ml_dtypes.float8_e4m3fn, 7), "e5m2": (ml_dtypes.float8_e5m2, 14)}[fmt]
    v = np.moveaxis(np.asarray(x, np.float32).astype(ml_dtypes.bfloat16).astype(np.float64), axis, -1)
    blocks = v.reshape(v.shape[:-1] + (-1, 32))
    amax = np.abs(blocks).max(-1, keepdims=True)
    byte = np.maximum(np.where(amax > 0, np.frexp(amax)[1] - 1 + 127, 0) - down, 1)
    scale = np.exp2(byte - 127.0)
    codes = (blocks / scale).astype(np.float32).astype(dtype).astype(np.float64)
    return np.moveaxis((codes * scale).reshape(v.shape), -1, axis)


WIDE = False


def mx_kscale(k):
    if not WIDE:
        return np.ones(k)
    levels = np.array([10, -10, 5, -5, 0])
    if k % 512:
        return np.exp2(np.random.permutation(np.resize(levels, k // 32))).repeat(32)
    a = np.empty((k // 512, 16))
    for p in range(k // 512):
        a[p, :8] = np.random.permutation(np.resize(levels, 8))
        for g in range(8):
            far = levels[np.abs(levels - a[p, g]) >= 10]
            a[p, g + 8] = far[np.random.randint(len(far))]
    return np.exp2(a.ravel()).repeat(32)


def f64(x):
    return np.asarray(x).astype(np.float64)


def striped(idx):
    return np.tile(idx.reshape(-1, 16).T, (8, 1)).astype(np.uint16)


def unstriped(offs):
    return offs[:16].T.reshape(-1).astype(np.int64)


def striped8(idx):
    return np.concatenate([x.reshape(-1, 16).T for x in idx]).astype(np.uint16)


def runs(offs, k):
    lists = np.stack([offs[16 * r : 16 * r + 16].T.reshape(-1) for r in range(8)]).astype(np.int64)
    return lists[np.arange(k) % 512 // 64]


def pack_weight(w):
    k, n = w.shape
    w = f64(np.asarray(w, np.float32).astype(ml_dtypes.bfloat16)).reshape(k // 32, 32, n)
    amax = np.abs(w).max(1)
    byte = np.clip(np.where(amax > 0, np.frexp(amax)[1] - 1 + 127 - 7, 1), 1, 254)
    scaled = (w * np.exp2(127.0 - byte)[:, None, :]).reshape(k, n).astype(np.float32)
    words = np.ascontiguousarray(scaled.reshape(k // 512, 128, 4, n).transpose(0, 1, 3, 2)).astype(ml_dtypes.float8_e4m3fn).view(np.uint8)
    return words, np.ascontiguousarray(byte.astype(np.uint8).reshape(k // 512, 16, n))


def unpack_weight(words, scales):
    g, p, n, _ = words.shape
    vals = np.ascontiguousarray(words).view(ml_dtypes.float8_e4m3fn).astype(np.float64) * np.repeat(np.exp2(scales.astype(np.float64) - 127.0), 8, axis=1)[..., None]
    return vals.transpose(0, 1, 3, 2).reshape(g * 512, n)


def sigmoid(v):
    return 1.0 / (1.0 + np.exp(-np.maximum(v, -700.0)))


K, T, S, V, N, H = 512, 2048, 1024, 512, 512, 512


def setup_inputs():
    n = np.random.standard_normal
    s = mx_kscale(K)[:, None]
    u = mx_kscale(H)
    packed_xT = pack_weight(n((K, T)) * s)
    return {
        "x_words": packed_xT[0],
        "x_scales": packed_xT[1],
        "w1": (n((K, H)) / np.sqrt(K) / s).astype(np.float32),
        "gn": (np.random.uniform(0.5, 1.5, (H, 1)) * u[:, None]).astype(np.float32),
        "w2": (n((H, N)) / np.sqrt(H) / u[:, None]).astype(np.float32),
        "offs": striped(np.random.permutation(T)[:S]),
        "n1": striped8(np.stack([np.random.permutation(S) for _ in range(8)])),
        "n2": striped8(np.stack([np.random.permutation(V) for _ in range(8)])),
        "n3": striped8(np.stack([np.random.permutation(V) for _ in range(8)])),
    }


def reference(x_words, x_scales, w1, gn, w2, offs, n1, n2, n3):
    xq = unpack_weight(x_words, x_scales)[:, unstriped(offs)]
    y = mxq(f64(w1), 0, "e4m3").T @ xq
    ln = y[np.arange(H)[:, None], runs(n1, H)]
    mx = ln.reshape(H, V, 2).max(axis=2)
    mn = ln.reshape(H, V, 2).min(axis=2)
    z = f64(gn) * (mx - (0.5 * mn))
    h = mxq(f64(w2), 0, "e4m3").T @ mxq(z, 0, "e4m3")
    sm = np.maximum(h, h[np.arange(N)[:, None], runs(n3, N)])
    ds = np.zeros((N, V))
    ds[np.arange(N)[:, None], runs(n2, N)] = sm
    return ds * sigmoid(h)

@@ -1,0 +1,244 @@
+from contextlib import ExitStack
+
+import concourse.mybir as mybir
+
+K, T, S, V, N, H = 512, 2048, 1024, 512, 512, 512
+FLOPS = 2 * K * H * S + 2 * H * N * V
+
+F32 = mybir.dt.float32
+BF16 = mybir.dt.bfloat16
+I32 = mybir.dt.int32
+U32 = mybir.dt.uint32
+U16 = mybir.dt.uint16
+U8 = mybir.dt.uint8
+FP8X4 = mybir.dt.float8_e4m3fn_x4
+ALU = mybir.AluOpType
+ACT = mybir.ActivationFunctionType
+
+P = 128
+PACK = 4
+HALVES = 2
+LIST_ROWS = 16
+
+
+def tile_picked_laypgapsendg_none_p_kernel(
+    tc, x_words, x_scales, w1, gn, w2, offs, n1, n2, n3, out
+):
+    nc = tc.nc
+    with ExitStack() as ctx:
+        keep = ctx.enter_context(tc.tile_pool(name="keep", bufs=1))
+        psum = ctx.enter_context(tc.psum_pool(name="psum", bufs=1))
+
+        def entries(list_tile, first, count):
+            return list_tile[:, first // LIST_ROWS : (first + count) // LIST_ROWS]
+
+        s_half = S // HALVES
+        v_half = V // HALVES
+        m_half = P // HALVES
+        c_half = H // HALVES
+
+        offs_t = keep.tile([P, S // LIST_ROWS], U16, name="offs_t")
+        n1_t = keep.tile([P, S // LIST_ROWS], U16, name="n1_t")
+        n2_t = keep.tile([P, V // LIST_ROWS], U16, name="n2_t")
+        n3_t = keep.tile([P, V // LIST_ROWS], U16, name="n3_t")
+        x_table = keep.tile([P, T], U32, name="x_table", align_bytes=64)
+        s_table = keep.tile([P, T], U8, name="s_table", align_bytes=64)
+        gain = keep.tile([P, PACK], F32, name="gain")
+
+        def load_weight_half(w, u):
+            raw = keep.tile([P, PACK, c_half], F32, name="w_raw", tag="w_raw%d" % u)
+            nc.sync.dma_start(raw[:], w.rearrange("(p j) c -> p j c", j=PACK)[:, :, u * c_half : (u + 1) * c_half])
+            return raw
+
+        def dealt_views(w_bf, raw, u):
+            return (
+                w_bf[:, :, u * m_half : (u + 1) * m_half, :].rearrange("p t m j -> p m t j"),
+                raw[:].rearrange("p j (m t) -> p m t j", t=PACK),
+            )
+
+        nc.vector.memset(s_table[:].bitcast(I32), 0)
+        nc.gpsimd.dma_start(gain[:], gn.rearrange("(p t) o -> p (t o)", t=PACK))
+        nc.sync.dma_start(offs_t[:], offs)
+        nc.sync.dma_start(n1_t[:], n1)
+        nc.sync.dma_start(n3_t[:], n3)
+        for q in range(4):
+            nc.scalar.dma_start(
+                s_table[32 * q : 32 * q + 4, :].bitcast(I32), x_scales[0, 4 * q : 4 * q + 4, :].bitcast(I32)
+            )
+        w1_raw = [load_weight_half(w1, u) for u in range(HALVES)]
+        nc.sync.dma_start(x_table[:].bitcast(I32), x_words[0].rearrange("p c r -> p (c r)").bitcast(I32))
+        nc.sync.dma_start(n2_t[:], n2)
+
+        half_gain = keep.tile([P, PACK], F32, name="half_gain")
+        positive = keep.tile([P, PACK], F32, name="positive")
+        slope = keep.tile([P, PACK], F32, name="slope")
+        factor = keep.tile([P, PACK], F32, name="factor")
+        nc.gpsimd.tensor_scalar(half_gain[:], gain[:], 0.5, 0.0, ALU.mult, ALU.add)
+        nc.gpsimd.tensor_scalar(positive[:], gain[:], 0.0, 1.0, ALU.is_ge, ALU.mult)
+        nc.gpsimd.tensor_scalar(slope[:], positive[:], 1.5, -2.0, ALU.mult, ALU.add)
+        nc.gpsimd.tensor_scalar(factor[:], positive[:], 3.0, -1.0, ALU.mult, ALU.add)
+
+        w1_bf = keep.tile([P, PACK, P, PACK], BF16, name="w1_bf", align_bytes=64)
+        for u in range(HALVES):
+            nc.scalar.copy(*dealt_views(w1_bf, w1_raw[u], u))
+        w2_raw = [load_weight_half(w2, u) for u in range(HALVES)]
+
+        picked_scales = keep.tile([P, S], U8, name="picked_scales", align_bytes=64)
+        nc.vector.tensor_copy(picked_scales[:], s_table[:].indirect(offs_t[:]))
+        w1_codes = keep.tile([P, H], U32, name="w1_codes", align_bytes=64)
+        w1_scales = keep.tile([P, H], U8, name="w1_scales", align_bytes=64)
+        nc.vector.quantize_mx(
+            out=w1_codes[:].bitcast(FP8X4), scales=w1_scales[:], in_=w1_bf[:].rearrange("p t m j -> p (t m j)")
+        )
+
+        y_rows = [keep.tile([P, S], F32, name="y_rows%d" % t) for t in range(PACK)]
+        picked_words = [keep.tile([P, s_half], U32, name="picked_words%d" % u, align_bytes=64) for u in range(HALVES)]
+        for u in range(HALVES):
+            nc.vector.tensor_copy(picked_words[u][:], x_table[:].indirect(entries(offs_t, u * s_half, s_half)))
+        y_banks = {}
+
+        def first_product(t, u):
+            y_banks[t, u] = psum.tile([P, s_half], F32, name="y_bank", tag="bank%d" % (HALVES * t + u))
+            nc.tensor.matmul_mx(
+                out=y_banks[t, u][:],
+                lhsT=w1_codes[:, t * P : (t + 1) * P].bitcast(FP8X4),
+                lhsT_scale=w1_scales[:, t * P : (t + 1) * P],
+                rhs=picked_words[u][:].bitcast(FP8X4),
+                rhs_scale=picked_scales[:, u * s_half : (u + 1) * s_half],
+                start=True,
+                stop=True,
+            )
+
+        def fetch_y(t, u):
+            place = y_rows[t][:, u * s_half : (u + 1) * s_half]
+            if u == 0:
+                nc.scalar.activation(place, y_banks[t, u][:], ACT.Copy, scale=half_gain[:, t : t + 1])
+            else:
+                nc.vector.tensor_scalar(place, y_banks[t, u][:], half_gain[:, t : t + 1], None, ALU.mult)
+
+        first_product(0, 0)
+        for t in range(PACK):
+            if t + 1 < PACK:
+                first_product(t + 1, 0)
+            first_product(t, 1)
+        for t in range(PACK):
+            if t + 1 < PACK:
+                fetch_y(t, 0)
+            fetch_y(t, 1)
+
+        w2_bf = keep.tile([P, PACK, P, PACK], BF16, name="w2_bf", align_bytes=64)
+        for u in range(HALVES):
+            nc.gpsimd.tensor_scalar(*dealt_views(w2_bf, w2_raw[u], u), 1.0, 0.0, ALU.mult, ALU.add)
+        w2_codes = keep.tile([P, N], U32, name="w2_codes", align_bytes=64)
+        w2_scales = keep.tile([P, N], U8, name="w2_scales", align_bytes=64)
+        nc.vector.quantize_mx(
+            out=w2_codes[:].bitcast(FP8X4), scales=w2_scales[:], in_=w2_bf[:].rearrange("p t m j -> p (t m j)")
+        )
+
+        z_planes = [keep.tile([P, PACK, v_half], F32, name="z_planes%d" % u) for u in range(HALVES)]
+        z_bf = [keep.tile([P, v_half, PACK], BF16, name="z_bf%d" % u, align_bytes=64) for u in range(HALVES)]
+        pieces = [(u, t) for u in range(HALVES) for t in range(PACK)]
+        lined, diff, kink, h_banks = {}, {}, {}, {}
+
+        def line_up(u, t):
+            lined[u, t] = keep.tile([P, v_half, 2], F32, name="lined%d_%d" % (u, t))
+            nc.scalar.activation(
+                lined[u, t][:].rearrange("p v e -> p (v e)"),
+                y_rows[t][:].indirect(entries(n1_t, u * s_half, s_half)),
+                ACT.Copy,
+            )
+            diff[u, t] = keep.tile([P, v_half], F32, name="diff%d_%d" % (u, t))
+            nc.vector.tensor_tensor(diff[u, t][:], lined[u, t][:, :, 1], lined[u, t][:, :, 0], ALU.subtract)
+
+        def bend(u, t):
+            kink[u, t] = keep.tile([P, v_half], F32, name="kink%d_%d" % (u, t))
+            nc.vector.scalar_tensor_tensor(
+                kink[u, t][:], diff[u, t][:], slope[:, t : t + 1], diff[u, t][:], ALU.mult, ALU.max
+            )
+
+        def finish_z(u, t):
+            nc.vector.scalar_tensor_tensor(
+                z_planes[u][:, t, :], kink[u, t][:], factor[:, t : t + 1], lined[u, t][:, :, 0], ALU.mult, ALU.add
+            )
+
+        def round_z(u):
+            nc.vector.tensor_copy(
+                z_bf[u][:].rearrange("p (c i) t -> p c t i", i=4), z_planes[u][:].rearrange("p t (c i) -> p c t i", i=4)
+            )
+
+        def second_product(u):
+            z_codes = keep.tile([P, v_half], U32, name="z_codes%d" % u, align_bytes=64)
+            z_scales = keep.tile([P, v_half], U8, name="z_scales%d" % u, align_bytes=64)
+            nc.vector.quantize_mx(
+                out=z_codes[:].bitcast(FP8X4), scales=z_scales[:], in_=z_bf[u][:].rearrange("p v t -> p (v t)")
+            )
+            for t in range(PACK):
+                h_banks[t, u] = psum.tile([P, v_half], F32, name="h_bank", tag="bank%d" % (HALVES * t + u))
+                nc.tensor.matmul_mx(
+                    out=h_banks[t, u][:],
+                    lhsT=w2_codes[:, t * P : (t + 1) * P].bitcast(FP8X4),
+                    lhsT_scale=w2_scales[:, t * P : (t + 1) * P],
+                    rhs=z_codes[:].bitcast(FP8X4),
+                    rhs_scale=z_scales[:],
+                    start=True,
+                    stop=True,
+                )
+
+        for n, piece in enumerate(pieces):
+            if n == 2:
+                fetch_y(PACK - 1, 0)
+            line_up(*piece)
+            if n > 0:
+                finish_z(*pieces[n - 1])
+            bend(*piece)
+            if n == PACK:
+                round_z(0)
+            if n == PACK + 1:
+                second_product(0)
+        finish_z(*pieces[-1])
+        round_z(1)
+        second_product(1)
+
+        h_rows = [keep.tile([P, V], F32, name="h_rows%d" % t) for t in range(PACK)]
+        out_rows = out.rearrange("(p t) v -> p t v", t=PACK)
+        sent = {}
+
+        def fetch_h(t, u):
+            nc.scalar.copy(h_rows[t][:, u * v_half : (u + 1) * v_half], h_banks[t, u][:])
+
+        def send(t):
+            partner = keep.tile([P, V], F32, name="partner%d" % t)
+            larger = keep.tile([P, V], F32, name="larger%d" % t)
+            for u in range(HALVES):
+                cols = slice(u * v_half, (u + 1) * v_half)
+                window = h_rows[t][:].indirect(entries(n3_t, u * v_half, v_half))
+                if (t, u) == (0, 0):
+                    nc.vector.tensor_copy(partner[:, cols], window)
+                else:
+                    nc.scalar.activation(partner[:, cols], window, ACT.Copy)
+            for u in range(HALVES):
+                cols = slice(u * v_half, (u + 1) * v_half)
+                nc.vector.tensor_tensor(larger[:, cols], h_banks[t, u][:], partner[:, cols], ALU.max)
+            sent[t] = keep.tile([P, 2 * V], F32, name="sent%d" % t)
+            nc.vector.tensor_copy(sent[t][:].indirect(n2_t[:]), larger[:])
+
+        def gate_and_store(t):
+            gate = keep.tile([P, V], F32, name="gate%d" % t)
+            nc.scalar.activation(gate[:], h_rows[t][:], ACT.Sigmoid)
+            result = keep.tile([P, V], F32, name="result%d" % t)
+            engine = nc.vector if t == PACK - 1 else nc.gpsimd
+            engine.tensor_tensor(result[:], sent[t][:, :V], gate[:], ALU.mult)
+            nc.sync.dma_start(out_rows[:, t, :], result[:])
+
+        for t in range(PACK):
+            fetch_h(t, 0)
+        fetch_h(0, 1)
+        fetch_h(1, 1)
+        send(0)
+        fetch_h(2, 1)
+        send(1)
+        fetch_h(3, 1)
+        for t in range(PACK):
+            if t + 2 < PACK:
+                send(t + 2)
+            gate_and_store(t)

@@ -78,9 +78,9 @@ def tile_picked_laypgapsendg_none_p_kernel(
         nc.gpsimd.tensor_scalar(slope[:], positive[:], 1.5, -2.0, ALU.mult, ALU.add)
         nc.gpsimd.tensor_scalar(factor[:], positive[:], 3.0, -1.0, ALU.mult, ALU.add)
 
-        w1_bf = keep.tile([P, PACK, P, PACK], BF16, name="w1_bf", align_bytes=64)
-        for u in range(HALVES):
-            nc.scalar.copy(*dealt_views(w1_bf, w1_raw[u], u))
+        w1_bf = keep.tile([P, PACK, P, PACK], BF16, name="w1_bf", tag="w1_bf", align_bytes=64)
+        nc.vector.tensor_copy(*dealt_views(w1_bf, w1_raw[0], 0))
+        nc.scalar.copy(*dealt_views(w1_bf, w1_raw[1], 1))
         w2_raw = [load_weight_half(w2, u) for u in range(HALVES)]
 
         picked_scales = keep.tile([P, S], U8, name="picked_scales", align_bytes=64)
@@ -92,9 +92,9 @@ def tile_picked_laypgapsendg_none_p_kernel(
         )
 
         y_rows = [keep.tile([P, S], F32, name="y_rows%d" % t) for t in range(PACK)]
-        picked_words = [keep.tile([P, s_half], U32, name="picked_words%d" % u, align_bytes=64) for u in range(HALVES)]
+        picked_words = keep.tile([P, S], U32, name="picked_words", tag="w1_bf", align_bytes=64)
         for u in range(HALVES):
-            nc.vector.tensor_copy(picked_words[u][:], x_table[:].indirect(entries(offs_t, u * s_half, s_half)))
+            nc.vector.tensor_copy(picked_words[:, u * s_half : (u + 1) * s_half], x_table[:].indirect(entries(offs_t, u * s_half, s_half)))
         y_banks = {}
 
         def first_product(t, u):
@@ -103,7 +103,7 @@ def tile_picked_laypgapsendg_none_p_kernel(
                 out=y_banks[t, u][:],
                 lhsT=w1_codes[:, t * P : (t + 1) * P].bitcast(FP8X4),
                 lhsT_scale=w1_scales[:, t * P : (t + 1) * P],
-                rhs=picked_words[u][:].bitcast(FP8X4),
+                rhs=picked_words[:, u * s_half : (u + 1) * s_half].bitcast(FP8X4),
                 rhs_scale=picked_scales[:, u * s_half : (u + 1) * s_half],
                 start=True,
                 stop=True,
@@ -129,53 +129,54 @@ def tile_picked_laypgapsendg_none_p_kernel(
         w2_bf = keep.tile([P, PACK, P, PACK], BF16, name="w2_bf", align_bytes=64)
         for u in range(HALVES):
             nc.gpsimd.tensor_scalar(*dealt_views(w2_bf, w2_raw[u], u), 1.0, 0.0, ALU.mult, ALU.add)
-        w2_codes = keep.tile([P, N], U32, name="w2_codes", align_bytes=64)
-        w2_scales = keep.tile([P, N], U8, name="w2_scales", align_bytes=64)
-        nc.vector.quantize_mx(
-            out=w2_codes[:].bitcast(FP8X4), scales=w2_scales[:], in_=w2_bf[:].rearrange("p t m j -> p (t m j)")
-        )
 
+        blocks = [(0, V // 2), (V // 2, V // 4), (3 * V // 4, V // 4)]
+        pieces = [(t, 0, v_half) for t in range(PACK)] + [(t, v_half, v_half) for t in range(PACK - 1)]
+        pieces = pieces + [(PACK - 1, first, count) for first, count in blocks[1:]]
         z_planes = [keep.tile([P, PACK, v_half], F32, name="z_planes%d" % u) for u in range(HALVES)]
-        z_bf = [keep.tile([P, v_half, PACK], BF16, name="z_bf%d" % u, align_bytes=64) for u in range(HALVES)]
-        pieces = [(u, t) for u in range(HALVES) for t in range(PACK)]
-        lined, diff, kink, h_banks = {}, {}, {}, {}
+        h_banks = [psum.tile([P, V], F32, name="h_bank", tag="bank%d" % (HALVES * t)) for t in range(PACK)]
+        lined, diff, kink, z_bf = {}, {}, {}, {}
 
-        def line_up(u, t):
-            lined[u, t] = keep.tile([P, v_half, 2], F32, name="lined%d_%d" % (u, t))
+        def line_up(t, first, count):
+            lined[t, first] = keep.tile([P, count, 2], F32, name="lined", tag="lined%d_%d" % (t, first), align_bytes=64)
             nc.scalar.activation(
-                lined[u, t][:].rearrange("p v e -> p (v e)"),
-                y_rows[t][:].indirect(entries(n1_t, u * s_half, s_half)),
+                lined[t, first][:].rearrange("p v e -> p (v e)"),
+                y_rows[t][:].indirect(entries(n1_t, 2 * first, 2 * count)),
                 ACT.Copy,
             )
-            diff[u, t] = keep.tile([P, v_half], F32, name="diff%d_%d" % (u, t))
-            nc.vector.tensor_tensor(diff[u, t][:], lined[u, t][:, :, 1], lined[u, t][:, :, 0], ALU.subtract)
+            diff[t, first] = keep.tile([P, count], F32, name="diff%d_%d" % (t, first))
+            nc.vector.tensor_tensor(diff[t, first][:], lined[t, first][:, :, 1], lined[t, first][:, :, 0], ALU.subtract)
 
-        def bend(u, t):
-            kink[u, t] = keep.tile([P, v_half], F32, name="kink%d_%d" % (u, t))
+        def bend(t, first, count):
+            kink[t, first] = keep.tile([P, count], F32, name="kink%d_%d" % (t, first))
             nc.vector.scalar_tensor_tensor(
-                kink[u, t][:], diff[u, t][:], slope[:, t : t + 1], diff[u, t][:], ALU.mult, ALU.max
+                kink[t, first][:], diff[t, first][:], slope[:, t : t + 1], diff[t, first][:], ALU.mult, ALU.max
             )
 
-        def finish_z(u, t):
+        def finish_z(t, first, count):
+            u, start = divmod(first, v_half)
             nc.vector.scalar_tensor_tensor(
-                z_planes[u][:, t, :], kink[u, t][:], factor[:, t : t + 1], lined[u, t][:, :, 0], ALU.mult, ALU.add
+                z_planes[u][:, t, start : start + count], kink[t, first][:], factor[:, t : t + 1],
+                lined[t, first][:, :, 0], ALU.mult, ALU.add,
             )
 
-        def round_z(u):
+        def round_z(first, count):
+            u, start = divmod(first, v_half)
+            z_bf[first] = keep.tile([P, count, PACK], BF16, name="z_bf%d" % first, align_bytes=64)
             nc.vector.tensor_copy(
-                z_bf[u][:].rearrange("p (c i) t -> p c t i", i=4), z_planes[u][:].rearrange("p t (c i) -> p c t i", i=4)
+                z_bf[first][:].rearrange("p (c i) t -> p c t i", i=4),
+                z_planes[u][:, :, start : start + count].rearrange("p t (c i) -> p c t i", i=4),
             )
 
-        def second_product(u):
-            z_codes = keep.tile([P, v_half], U32, name="z_codes%d" % u, align_bytes=64)
-            z_scales = keep.tile([P, v_half], U8, name="z_scales%d" % u, align_bytes=64)
+        def second_product(w2_codes, w2_scales, first, count):
+            z_codes = keep.tile([P, count], U32, name="z_codes%d" % first, align_bytes=64)
+            z_scales = keep.tile([P, count], U8, name="z_scales%d" % first, align_bytes=64)
             nc.vector.quantize_mx(
-                out=z_codes[:].bitcast(FP8X4), scales=z_scales[:], in_=z_bf[u][:].rearrange("p v t -> p (v t)")
+                out=z_codes[:].bitcast(FP8X4), scales=z_scales[:], in_=z_bf[first][:].rearrange("p v t -> p (v t)")
             )
             for t in range(PACK):
-                h_banks[t, u] = psum.tile([P, v_half], F32, name="h_bank", tag="bank%d" % (HALVES * t + u))
                 nc.tensor.matmul_mx(
-                    out=h_banks[t, u][:],
+                    out=h_banks[t][:, first : first + count],
                     lhsT=w2_codes[:, t * P : (t + 1) * P].bitcast(FP8X4),
                     lhsT_scale=w2_scales[:, t * P : (t + 1) * P],
                     rhs=z_codes[:].bitcast(FP8X4),
@@ -184,6 +185,18 @@ def tile_picked_laypgapsendg_none_p_kernel(
                     stop=True,
                 )
 
+        h_rows = [keep.tile([P, V], F32, name="h_rows", tag="h_rows%d" % t) for t in range(PACK)]
+
+        def fetch_h(t, first, count):
+            nc.scalar.copy(h_rows[t][:, first : first + count], h_banks[t][:, first : first + count])
+
+        gates = {}
+
+        def squash(t, first, count, tag):
+            if t not in gates:
+                gates[t] = keep.tile([P, V], F32, name="gate", tag=tag)
+            nc.scalar.activation(gates[t][:, first : first + count], h_rows[t][:, first : first + count], ACT.Sigmoid)
+
         for n, piece in enumerate(pieces):
             if n == 2:
                 fetch_y(PACK - 1, 0)
@@ -191,54 +204,78 @@ def tile_picked_laypgapsendg_none_p_kernel(
             if n > 0:
                 finish_z(*pieces[n - 1])
             bend(*piece)
+            if n == 1:
+                w2_codes = keep.tile([P, N], U32, name="w2_codes", tag="lined0_0", align_bytes=64)
+                w2_scales = keep.tile([P, N], U8, name="w2_scales", align_bytes=64)
+                nc.vector.quantize_mx(
+                    out=w2_codes[:].bitcast(FP8X4), scales=w2_scales[:], in_=w2_bf[:].rearrange("p t m j -> p (t m j)")
+                )
             if n == PACK:
-                round_z(0)
+                round_z(*blocks[0])
             if n == PACK + 1:
-                second_product(0)
+                second_product(w2_codes, w2_scales, *blocks[0])
+        for t in range(PACK):
+            fetch_h(t, *blocks[0])
+        squash(PACK - 1, 0, v_half, "gate3")
+        round_z(*blocks[1])
         finish_z(*pieces[-1])
-        round_z(1)
-        second_product(1)
+        second_product(w2_codes, w2_scales, *blocks[1])
+        round_z(*blocks[2])
+        second_product(w2_codes, w2_scales, *blocks[2])
+        fetch_h(0, v_half, v_half)
 
-        h_rows = [keep.tile([P, V], F32, name="h_rows%d" % t) for t in range(PACK)]
         out_rows = out.rearrange("(p t) v -> p t v", t=PACK)
-        sent = {}
+        halves = [slice(u * v_half, (u + 1) * v_half) for u in range(HALVES)]
+        partner = [keep.tile([P, V], F32, name="partner%d" % t) for t in range(PACK)]
+        larger = [keep.tile([P, V], F32, name="larger%d" % t) for t in range(PACK)]
+        sent = [keep.tile([P, 2 * V], F32, name="sent%d" % t) for t in range(PACK)]
 
-        def fetch_h(t, u):
-            nc.scalar.copy(h_rows[t][:, u * v_half : (u + 1) * v_half], h_banks[t, u][:])
+        def partner_window(t, u):
+            return h_rows[t][:].indirect(entries(n3_t, u * v_half, v_half))
+
+        def fetch_partner(t, u):
+            nc.scalar.activation(partner[t][:, halves[u]], partner_window(t, u), ACT.Copy)
+
+        def larger_on_vector(t):
+            nc.vector.tensor_tensor(larger[t][:], h_banks[t][:], partner[t][:], ALU.max)
+
+        def larger_on_gpsimd(t):
+            excess = keep.tile([P, V], F32, name="excess", tag="excess%d" % t)
+            lift = keep.tile([P, V], F32, name="lift", tag="lift%d" % t)
+            nc.gpsimd.tensor_tensor(excess[:], partner[t][:], h_rows[t][:], ALU.subtract)
+            nc.scalar.activation(lift[:], excess[:], ACT.Relu)
+            nc.gpsimd.tensor_tensor(larger[t][:], h_rows[t][:], lift[:], ALU.add)
 
         def send(t):
-            partner = keep.tile([P, V], F32, name="partner%d" % t)
-            larger = keep.tile([P, V], F32, name="larger%d" % t)
-            for u in range(HALVES):
-                cols = slice(u * v_half, (u + 1) * v_half)
-                window = h_rows[t][:].indirect(entries(n3_t, u * v_half, v_half))
-                if (t, u) == (0, 0):
-                    nc.vector.tensor_copy(partner[:, cols], window)
-                else:
-                    nc.scalar.activation(partner[:, cols], window, ACT.Copy)
-            for u in range(HALVES):
-                cols = slice(u * v_half, (u + 1) * v_half)
-                nc.vector.tensor_tensor(larger[:, cols], h_banks[t, u][:], partner[:, cols], ALU.max)
-            sent[t] = keep.tile([P, 2 * V], F32, name="sent%d" % t)
-            nc.vector.tensor_copy(sent[t][:].indirect(n2_t[:]), larger[:])
+            nc.vector.tensor_copy(sent[t][:].indirect(n2_t[:]), larger[t][:])
 
-        def gate_and_store(t):
-            gate = keep.tile([P, V], F32, name="gate%d" % t)
-            nc.scalar.activation(gate[:], h_rows[t][:], ACT.Sigmoid)
-            result = keep.tile([P, V], F32, name="result%d" % t)
-            engine = nc.vector if t == PACK - 1 else nc.gpsimd
-            engine.tensor_tensor(result[:], sent[t][:, :V], gate[:], ALU.mult)
+        def gate_and_store(t, tag):
+            result = keep.tile([P, V], F32, name="result", tag=tag)
+            nc.gpsimd.tensor_tensor(result[:], sent[t][:, :V], gates[t][:], ALU.mult)
             nc.sync.dma_start(out_rows[:, t, :], result[:])
 
-        for t in range(PACK):
-            fetch_h(t, 0)
-        fetch_h(0, 1)
-        fetch_h(1, 1)
+        nc.vector.tensor_copy(partner[0][:, halves[0]], partner_window(0, 0))
+        fetch_partner(0, 1)
+        larger_on_vector(0)
+        squash(0, 0, V, "gate0")
         send(0)
-        fetch_h(2, 1)
-        send(1)
-        fetch_h(3, 1)
-        for t in range(PACK):
-            if t + 2 < PACK:
-                send(t + 2)
-            gate_and_store(t)
+        for t in range(1, PACK):
+            fetch_h(t, v_half, v_half)
+            for u in range(HALVES):
+                fetch_partner(t, u)
+            if t == 1:
+                larger_on_vector(t)
+            else:
+                larger_on_gpsimd(t)
+            send(t)
+        last = PACK - 1
+        for t in range(1, last):
+            squash(t, 0, V, "excess%d" % (t + 1))
+        squash(last, v_half, v_half, "gate3")
+        gate_and_store(0, "lift2")
+        gate_and_store(1, "lift3")
+        gate_and_store(2, "h_rows3")
+        for u, cols in enumerate(halves):
+            result = keep.tile([P, v_half], F32, name="last_result%d" % u)
+            nc.vector.tensor_tensor(result[:], sent[last][:, cols], gates[last][:, cols], ALU.mult)
+            nc.scalar.dma_start(out_rows[:, last, cols], result[:])

from contextlib import ExitStack

import concourse.mybir as mybir

K, T, S, V, N, H = 512, 2048, 1024, 512, 512, 512
FLOPS = 2 * K * H * S + 2 * H * N * V

F32 = mybir.dt.float32
BF16 = mybir.dt.bfloat16
I32 = mybir.dt.int32
U32 = mybir.dt.uint32
U16 = mybir.dt.uint16
U8 = mybir.dt.uint8
FP8X4 = mybir.dt.float8_e4m3fn_x4
ALU = mybir.AluOpType
ACT = mybir.ActivationFunctionType

P = 128
PACK = 4
HALVES = 2
LIST_ROWS = 16


def tile_picked_laypgapsendg_none_p_kernel(
    tc, x_words, x_scales, w1, gn, w2, offs, n1, n2, n3, out
):
    nc = tc.nc
    with ExitStack() as ctx:
        keep = ctx.enter_context(tc.tile_pool(name="keep", bufs=1))
        psum = ctx.enter_context(tc.psum_pool(name="psum", bufs=1))

        def entries(list_tile, first, count):
            return list_tile[:, first // LIST_ROWS : (first + count) // LIST_ROWS]

        s_half = S // HALVES
        v_half = V // HALVES
        m_half = P // HALVES
        c_half = H // HALVES

        offs_t = keep.tile([P, S // LIST_ROWS], U16, name="offs_t")
        n1_t = keep.tile([P, S // LIST_ROWS], U16, name="n1_t")
        n2_t = keep.tile([P, V // LIST_ROWS], U16, name="n2_t")
        n3_t = keep.tile([P, V // LIST_ROWS], U16, name="n3_t")
        x_table = keep.tile([P, T], U32, name="x_table", align_bytes=64)
        s_table = keep.tile([P, T], U8, name="s_table", align_bytes=64)
        gain = keep.tile([P, PACK], F32, name="gain")

        def load_weight_half(w, u):
            raw = keep.tile([P, PACK, c_half], F32, name="w_raw", tag="w_raw%d" % u)
            nc.sync.dma_start(raw[:], w.rearrange("(p j) c -> p j c", j=PACK)[:, :, u * c_half : (u + 1) * c_half])
            return raw

        def dealt_views(w_bf, raw, u):
            return (
                w_bf[:, :, u * m_half : (u + 1) * m_half, :].rearrange("p t m j -> p m t j"),
                raw[:].rearrange("p j (m t) -> p m t j", t=PACK),
            )

        nc.vector.memset(s_table[:].bitcast(I32), 0)
        nc.gpsimd.dma_start(gain[:], gn.rearrange("(p t) o -> p (t o)", t=PACK))
        nc.sync.dma_start(offs_t[:], offs)
        nc.sync.dma_start(n1_t[:], n1)
        nc.sync.dma_start(n3_t[:], n3)
        for q in range(4):
            nc.scalar.dma_start(
                s_table[32 * q : 32 * q + 4, :].bitcast(I32), x_scales[0, 4 * q : 4 * q + 4, :].bitcast(I32)
            )
        w1_raw = [load_weight_half(w1, u) for u in range(HALVES)]
        nc.sync.dma_start(x_table[:].bitcast(I32), x_words[0].rearrange("p c r -> p (c r)").bitcast(I32))
        nc.sync.dma_start(n2_t[:], n2)

        half_gain = keep.tile([P, PACK], F32, name="half_gain")
        positive = keep.tile([P, PACK], F32, name="positive")
        slope = keep.tile([P, PACK], F32, name="slope")
        factor = keep.tile([P, PACK], F32, name="factor")
        nc.gpsimd.tensor_scalar(half_gain[:], gain[:], 0.5, 0.0, ALU.mult, ALU.add)
        nc.gpsimd.tensor_scalar(positive[:], gain[:], 0.0, 1.0, ALU.is_ge, ALU.mult)
        nc.gpsimd.tensor_scalar(slope[:], positive[:], 1.5, -2.0, ALU.mult, ALU.add)
        nc.gpsimd.tensor_scalar(factor[:], positive[:], 3.0, -1.0, ALU.mult, ALU.add)

        w1_bf = keep.tile([P, PACK, P, PACK], BF16, name="w1_bf", tag="w1_bf", align_bytes=64)
        nc.vector.tensor_copy(*dealt_views(w1_bf, w1_raw[0], 0))
        nc.scalar.copy(*dealt_views(w1_bf, w1_raw[1], 1))
        w2_raw = [load_weight_half(w2, u) for u in range(HALVES)]

        picked_scales = keep.tile([P, S], U8, name="picked_scales", align_bytes=64)
        nc.vector.tensor_copy(picked_scales[:], s_table[:].indirect(offs_t[:]))
        w1_codes = keep.tile([P, H], U32, name="w1_codes", align_bytes=64)
        w1_scales = keep.tile([P, H], U8, name="w1_scales", align_bytes=64)
        nc.vector.quantize_mx(
            out=w1_codes[:].bitcast(FP8X4), scales=w1_scales[:], in_=w1_bf[:].rearrange("p t m j -> p (t m j)")
        )

        y_rows = [keep.tile([P, S], F32, name="y_rows%d" % t) for t in range(PACK)]
        picked_words = keep.tile([P, S], U32, name="picked_words", tag="w1_bf", align_bytes=64)
        for u in range(HALVES):
            nc.vector.tensor_copy(picked_words[:, u * s_half : (u + 1) * s_half], x_table[:].indirect(entries(offs_t, u * s_half, s_half)))
        y_banks = {}

        def first_product(t, u):
            y_banks[t, u] = psum.tile([P, s_half], F32, name="y_bank", tag="bank%d" % (HALVES * t + u))
            nc.tensor.matmul_mx(
                out=y_banks[t, u][:],
                lhsT=w1_codes[:, t * P : (t + 1) * P].bitcast(FP8X4),
                lhsT_scale=w1_scales[:, t * P : (t + 1) * P],
                rhs=picked_words[:, u * s_half : (u + 1) * s_half].bitcast(FP8X4),
                rhs_scale=picked_scales[:, u * s_half : (u + 1) * s_half],
                start=True,
                stop=True,
            )

        def fetch_y(t, u):
            place = y_rows[t][:, u * s_half : (u + 1) * s_half]
            if u == 0:
                nc.scalar.activation(place, y_banks[t, u][:], ACT.Copy, scale=half_gain[:, t : t + 1])
            else:
                nc.vector.tensor_scalar(place, y_banks[t, u][:], half_gain[:, t : t + 1], None, ALU.mult)

        first_product(0, 0)
        for t in range(PACK):
            if t + 1 < PACK:
                first_product(t + 1, 0)
            first_product(t, 1)
        for t in range(PACK):
            if t + 1 < PACK:
                fetch_y(t, 0)
            fetch_y(t, 1)

        w2_bf = keep.tile([P, PACK, P, PACK], BF16, name="w2_bf", align_bytes=64)
        for u in range(HALVES):
            nc.gpsimd.tensor_scalar(*dealt_views(w2_bf, w2_raw[u], u), 1.0, 0.0, ALU.mult, ALU.add)

        blocks = [(0, V // 2), (V // 2, V // 4), (3 * V // 4, V // 4)]
        pieces = [(t, 0, v_half) for t in range(PACK)] + [(t, v_half, v_half) for t in range(PACK - 1)]
        pieces = pieces + [(PACK - 1, first, count) for first, count in blocks[1:]]
        z_planes = [keep.tile([P, PACK, v_half], F32, name="z_planes%d" % u) for u in range(HALVES)]
        h_banks = [psum.tile([P, V], F32, name="h_bank", tag="bank%d" % (HALVES * t)) for t in range(PACK)]
        lined, diff, kink, z_bf = {}, {}, {}, {}

        def line_up(t, first, count):
            lined[t, first] = keep.tile([P, count, 2], F32, name="lined", tag="lined%d_%d" % (t, first), align_bytes=64)
            nc.scalar.activation(
                lined[t, first][:].rearrange("p v e -> p (v e)"),
                y_rows[t][:].indirect(entries(n1_t, 2 * first, 2 * count)),
                ACT.Copy,
            )
            diff[t, first] = keep.tile([P, count], F32, name="diff%d_%d" % (t, first))
            nc.vector.tensor_tensor(diff[t, first][:], lined[t, first][:, :, 1], lined[t, first][:, :, 0], ALU.subtract)

        def bend(t, first, count):
            kink[t, first] = keep.tile([P, count], F32, name="kink%d_%d" % (t, first))
            nc.vector.scalar_tensor_tensor(
                kink[t, first][:], diff[t, first][:], slope[:, t : t + 1], diff[t, first][:], ALU.mult, ALU.max
            )

        def finish_z(t, first, count):
            u, start = divmod(first, v_half)
            nc.vector.scalar_tensor_tensor(
                z_planes[u][:, t, start : start + count], kink[t, first][:], factor[:, t : t + 1],
                lined[t, first][:, :, 0], ALU.mult, ALU.add,
            )

        def round_z(first, count):
            u, start = divmod(first, v_half)
            z_bf[first] = keep.tile([P, count, PACK], BF16, name="z_bf%d" % first, align_bytes=64)
            nc.vector.tensor_copy(
                z_bf[first][:].rearrange("p (c i) t -> p c t i", i=4),
                z_planes[u][:, :, start : start + count].rearrange("p t (c i) -> p c t i", i=4),
            )

        def second_product(w2_codes, w2_scales, first, count):
            z_codes = keep.tile([P, count], U32, name="z_codes%d" % first, align_bytes=64)
            z_scales = keep.tile([P, count], U8, name="z_scales%d" % first, align_bytes=64)
            nc.vector.quantize_mx(
                out=z_codes[:].bitcast(FP8X4), scales=z_scales[:], in_=z_bf[first][:].rearrange("p v t -> p (v t)")
            )
            for t in range(PACK):
                nc.tensor.matmul_mx(
                    out=h_banks[t][:, first : first + count],
                    lhsT=w2_codes[:, t * P : (t + 1) * P].bitcast(FP8X4),
                    lhsT_scale=w2_scales[:, t * P : (t + 1) * P],
                    rhs=z_codes[:].bitcast(FP8X4),
                    rhs_scale=z_scales[:],
                    start=True,
                    stop=True,
                )

        h_rows = [keep.tile([P, V], F32, name="h_rows", tag="h_rows%d" % t) for t in range(PACK)]

        def fetch_h(t, first, count):
            nc.scalar.copy(h_rows[t][:, first : first + count], h_banks[t][:, first : first + count])

        gates = {}

        def squash(t, first, count, tag):
            if t not in gates:
                gates[t] = keep.tile([P, V], F32, name="gate", tag=tag)
            nc.scalar.activation(gates[t][:, first : first + count], h_rows[t][:, first : first + count], ACT.Sigmoid)

        for n, piece in enumerate(pieces):
            if n == 2:
                fetch_y(PACK - 1, 0)
            line_up(*piece)
            if n > 0:
                finish_z(*pieces[n - 1])
            bend(*piece)
            if n == 1:
                w2_codes = keep.tile([P, N], U32, name="w2_codes", tag="lined0_0", align_bytes=64)
                w2_scales = keep.tile([P, N], U8, name="w2_scales", align_bytes=64)
                nc.vector.quantize_mx(
                    out=w2_codes[:].bitcast(FP8X4), scales=w2_scales[:], in_=w2_bf[:].rearrange("p t m j -> p (t m j)")
                )
            if n == PACK:
                round_z(*blocks[0])
            if n == PACK + 1:
                second_product(w2_codes, w2_scales, *blocks[0])
        for t in range(PACK):
            fetch_h(t, *blocks[0])
        squash(PACK - 1, 0, v_half, "gate3")
        round_z(*blocks[1])
        finish_z(*pieces[-1])
        second_product(w2_codes, w2_scales, *blocks[1])
        round_z(*blocks[2])
        second_product(w2_codes, w2_scales, *blocks[2])
        fetch_h(0, v_half, v_half)

        out_rows = out.rearrange("(p t) v -> p t v", t=PACK)
        halves = [slice(u * v_half, (u + 1) * v_half) for u in range(HALVES)]
        partner = [keep.tile([P, V], F32, name="partner%d" % t) for t in range(PACK)]
        larger = [keep.tile([P, V], F32, name="larger%d" % t) for t in range(PACK)]
        sent = [keep.tile([P, 2 * V], F32, name="sent%d" % t) for t in range(PACK)]

        def partner_window(t, u):
            return h_rows[t][:].indirect(entries(n3_t, u * v_half, v_half))

        def fetch_partner(t, u):
            nc.scalar.activation(partner[t][:, halves[u]], partner_window(t, u), ACT.Copy)

        def larger_on_vector(t):
            nc.vector.tensor_tensor(larger[t][:], h_banks[t][:], partner[t][:], ALU.max)

        def larger_on_gpsimd(t):
            excess = keep.tile([P, V], F32, name="excess", tag="excess%d" % t)
            lift = keep.tile([P, V], F32, name="lift", tag="lift%d" % t)
            nc.gpsimd.tensor_tensor(excess[:], partner[t][:], h_rows[t][:], ALU.subtract)
            nc.scalar.activation(lift[:], excess[:], ACT.Relu)
            nc.gpsimd.tensor_tensor(larger[t][:], h_rows[t][:], lift[:], ALU.add)

        def send(t):
            nc.vector.tensor_copy(sent[t][:].indirect(n2_t[:]), larger[t][:])

        def gate_and_store(t, tag):
            result = keep.tile([P, V], F32, name="result", tag=tag)
            nc.gpsimd.tensor_tensor(result[:], sent[t][:, :V], gates[t][:], ALU.mult)
            nc.sync.dma_start(out_rows[:, t, :], result[:])

        nc.vector.tensor_copy(partner[0][:, halves[0]], partner_window(0, 0))
        fetch_partner(0, 1)
        larger_on_vector(0)
        squash(0, 0, V, "gate0")
        send(0)
        for t in range(1, PACK):
            fetch_h(t, v_half, v_half)
            for u in range(HALVES):
                fetch_partner(t, u)
            if t == 1:
                larger_on_vector(t)
            else:
                larger_on_gpsimd(t)
            send(t)
        last = PACK - 1
        for t in range(1, last):
            squash(t, 0, V, "excess%d" % (t + 1))
        squash(last, v_half, v_half, "gate3")
        gate_and_store(0, "lift2")
        gate_and_store(1, "lift3")
        gate_and_store(2, "h_rows3")
        for u, cols in enumerate(halves):
            result = keep.tile([P, v_half], F32, name="last_result%d" % u)
            nc.vector.tensor_tensor(result[:], sent[last][:, cols], gates[last][:, cols], ALU.mult)
            nc.scalar.dma_start(out_rows[:, last, cols], result[:])
